import numpy as np
import ml_dtypes


def mxq(x, axis, fmt="e4m3"):
    dtype, down = {"e4m3": (ml_dtypes.float8_e4m3fn, 7), "e5m2": (ml_dtypes.float8_e5m2, 14)}[fmt]
    v = np.moveaxis(np.asarray(x, np.float32).astype(ml_dtypes.bfloat16).astype(np.float64), axis, -1)
    blocks = v.reshape(v.shape[:-1] + (-1, 32))
    amax = np.abs(blocks).max(-1, keepdims=True)
    byte = np.maximum(np.where(amax > 0, np.frexp(amax)[1] - 1 + 127, 0) - down, 1)
    scale = np.exp2(byte - 127.0)
    codes = (blocks / scale).astype(np.float32).astype(dtype).astype(np.float64)
    return np.moveaxis((codes * scale).reshape(v.shape), -1, axis)


WIDE = False


def mx_kscale(k):
    if not WIDE:
        return np.ones(k)
    levels = np.array([10, -10, 5, -5, 0])
    if k % 512:
        return np.exp2(np.random.permutation(np.resize(levels, k // 32))).repeat(32)
    a = np.empty((k // 512, 16))
    for p in range(k // 512):
        a[p, :8] = np.random.permutation(np.resize(levels, 8))
        for g in range(8):
            far = levels[np.abs(levels - a[p, g]) >= 10]
            a[p, g + 8] = far[np.random.randint(len(far))]
    return np.exp2(a.ravel()).repeat(32)


def f64(x):
    return np.asarray(x).astype(np.float64)


def striped(idx):
    return np.tile(np.asarray(idx).reshape(-1, 16).T, (8, 1)).astype(np.uint16)


def unstriped(offs):
    return offs[:16].T.reshape(-1).astype(np.int64)


B, N, T, D, DV, NQ = 1, 512, 1024, 1024, 256, 128


def setup_inputs():
    n = np.random.standard_normal
    idx = np.random.permutation(T)[:B * N]
    s = mx_kscale(D)[:, None]
    u = np.ones(T)
    u[idx] = mx_kscale(B * N)
    r = np.random.uniform(0.5, 2.0, T)
    k = n((D, T)) / s
    v = n((DV, T)) / (u * r)
    return {
        "qT": (n((B, D, NQ)) * s * (0.60 / np.sqrt(D))).astype(np.float32),
        "kT": k.astype(np.float32),
        "vT": v.astype(np.float32),
        "vs": np.tile(u * r, (128, 1)).astype(np.float32),
        "offs": striped(idx),
    }


def reference(qT, kT, vT, vs, offs):
    idx = unstriped(offs)
    k = f64(kT)
    v = f64(vT)
    pick = lambda x: x[:, idx].reshape(x.shape[0], B, N).transpose(1, 0, 2)
    q = f64(qT)
    score = mxq(q, 1, "e4m3").transpose(0, 2, 1) @ mxq(pick(k), 1, "e4m3")
    m = score.max(-1, keepdims=True)
    p = np.exp(score - m)
    total = p.sum(-1, keepdims=True)
    w = p * pick(f64(vs))[:, :1, :]
    y = mxq(w, 2, "e4m3") @ mxq(pick(v).transpose(0, 2, 1), 1, "e4m3")
    y = y / total
    return y

@@ -1,0 +1,218 @@
+from contextlib import ExitStack
+
+import concourse.mybir as mybir
+from concourse.masks import make_identity
+
+F32 = mybir.dt.float32
+BF16 = mybir.dt.bfloat16
+U32 = mybir.dt.uint32
+U16 = mybir.dt.uint16
+U8 = mybir.dt.uint8
+FP8X4 = mybir.dt.float8_e4m3fn_x4
+ACT = mybir.ActivationFunctionType
+ALU = mybir.AluOpType
+AXIS = mybir.AxisListType
+
+P = 128
+N, T, DK, DV, NQ = 512, 1024, 1024, 256, 128
+PASSES = DK // 512
+HALF = T // 2
+
+FLOPS = 2 * NQ * N * (DK + DV)
+BYTES = 4 * (DK * NQ + DK * T + DV * T + T + NQ * DV) + 2 * P * N // 16
+
+
+def tile_attend_knn_kernel(tc, qT, kT, vT, vs, offs, out):
+    nc = tc.nc
+    with ExitStack() as ctx:
+        keep = ctx.enter_context(tc.tile_pool(name="keep", bufs=1))
+        psum = ctx.enter_context(tc.psum_pool(name="psum", bufs=1))
+
+        offsets = keep.tile([P, N // 16], U16, name="offsets")
+        nc.sync.dma_start(offsets[:], offs)
+
+        warm = keep.tile([P, 1], F32, name="warm")
+        warm_out = keep.tile([P, 1], F32, name="warm_out")
+        nc.vector.memset(warm[:], 0.0)
+        nc.scalar.activation(out=warm_out[:], in_=warm[:], func=ACT.Exp)
+
+        vs_pool = keep.tile([P, T], F32, name="vs_pool")
+        nc.gpsimd.memset(vs_pool[:], 0.0)
+        nc.scalar.dma_start(out=vs_pool[0:1, :], in_=vs[0:1, :])
+        ident32 = keep.tile([P, P], F32, name="ident32")
+        make_identity(nc, ident32[:])
+
+        kraw = {}
+
+        def load_keys(g, u, h):
+            raw = keep.tile([P, 2, HALF], F32, name=f"kraw_{g}_{u}_{h}")
+            rows = kT[512 * g : 512 * (g + 1), HALF * h : HALF * (h + 1)]
+            rows = rows.rearrange("(p u e) n -> p u e n", u=2, e=2)
+            nc.sync.dma_start(out=raw[:], in_=rows[:, u, :, :])
+            kraw[g, u, h] = raw
+
+        qraw = {}
+
+        def load_queries(g):
+            raw = keep.tile([P, 4, NQ], F32, name=f"qraw_{g}")
+            rows = qT[0, 512 * g : 512 * (g + 1), :]
+            nc.sync.dma_start(out=raw[:], in_=rows.rearrange("(p j) q -> p j q", j=4))
+            qraw[g] = raw
+
+        vraw = {}
+
+        def load_values(h):
+            raw = keep.tile([P, 2, HALF], F32, name=f"vraw_{h}")
+            cols = vT[:, HALF * h : HALF * (h + 1)]
+            nc.sync.dma_start(out=raw[:], in_=cols.rearrange("(p u) n -> p u n", u=2))
+            vraw[h] = raw
+
+        load_keys(0, 0, 0)
+        load_keys(0, 0, 1)
+        load_keys(0, 1, 0)
+        load_keys(0, 1, 1)
+        load_keys(1, 0, 0)
+        load_keys(1, 0, 1)
+        load_keys(1, 1, 0)
+        load_keys(1, 1, 1)
+        load_queries(0)
+        load_queries(1)
+        load_values(0)
+        load_values(1)
+
+        kpool = {}
+        for g in range(PASSES):
+            for u in range(2):
+                kpool[g, u] = keep.tile([P, 2 * T], BF16, name=f"kpool_{g}_{u}", align_bytes=64)
+        vpool = keep.tile([P, 2 * T], BF16, name="vpool", align_bytes=64)
+
+        def cast(engine_copy, pool, raw, h, a, b):
+            dst = pool[:, 2 * (HALF * h + a) : 2 * (HALF * h + b)]
+            engine_copy(out=dst.rearrange("p (n e) -> p n e", e=2), in_=raw[:, :, a:b].rearrange("p e n -> p n e"))
+
+        kgrp = [keep.tile([P, 4 * N], BF16, name=f"kgrp_{g}", align_bytes=64) for g in range(PASSES)]
+        kcodes = [keep.tile([P, N], U32, name=f"kcodes_{g}", align_bytes=64) for g in range(PASSES)]
+        kscales = [keep.tile([P, N], U8, name=f"kscales_{g}", align_bytes=64) for g in range(PASSES)]
+
+        def gather_keys(g, u):
+            words = kgrp[g][:].bitcast(U32).rearrange("p (n u) -> p n u", u=2)
+            nc.vector.tensor_copy(out=words[:, :, u], in_=kpool[g, u][:].bitcast(U32).indirect(offsets[:]))
+
+        def quantize_keys(g):
+            nc.vector.quantize_mx(out=kcodes[g][:].bitcast(FP8X4), scales=kscales[g][:], in_=kgrp[g][:])
+
+        scores = psum.tile([P, N], F32, name="scores")
+        qcodes = keep.tile([P, PASSES * NQ], U32, name="qcodes", align_bytes=64)
+        qscales = keep.tile([P, PASSES * NQ], U8, name="qscales", align_bytes=64)
+        qgrp = keep.tile([P, PASSES, NQ, 4], BF16, name="qgrp", align_bytes=64)
+
+        def cast_queries(engine_copy, g):
+            engine_copy(out=qgrp[:, g, :, :], in_=qraw[g][:].rearrange("p j q -> p q j"))
+
+        def score_pass(g):
+            nc.tensor.matmul_mx(
+                out=scores[:],
+                lhsT=qcodes[:, NQ * g : NQ * (g + 1)].bitcast(FP8X4),
+                lhsT_scale=qscales[:, NQ * g : NQ * (g + 1)],
+                rhs=kcodes[g][:].bitcast(FP8X4),
+                rhs_scale=kscales[g][:],
+                start=(g == 0),
+                stop=(g == PASSES - 1),
+            )
+
+        sc, ve = nc.scalar.copy, nc.vector.tensor_copy
+        vs_got = keep.tile([P, N], F32, name="vs_got")
+        vs_cols = keep.tile([P, 4], F32, name="vs_cols")
+        vs_turned = psum.tile([P, 4, P], F32, name="vs_turned")
+
+        nc.vector.tensor_copy(out=vs_got[:], in_=vs_pool[:].indirect(offsets[:]))
+        vs_by_slot = vs_got[:].rearrange("p (s t) -> p t s", t=4)
+        for t in range(4):
+            nc.tensor.transpose(vs_turned[:, t, :], vs_by_slot[:, t, :], ident32[:])
+        cuts = {(0, 0, 0): 0, (0, 0, 1): 256, (0, 1, 0): 0, (0, 1, 1): 256, (1, 0, 0): 0, (1, 0, 1): 256, (1, 1, 0): 0, (1, 1, 1): 320}
+        for g in range(PASSES):
+            for u in range(2):
+                for h in range(2):
+                    cut = cuts[g, u, h]
+                    if cut < HALF:
+                        cast(sc, kpool[g, u], kraw[g, u, h], h, cut, HALF)
+                    if cut > 0:
+                        cast(ve, kpool[g, u], kraw[g, u, h], h, 0, cut)
+                if (g, u) == (0, 1):
+                    nc.vector.tensor_copy(out=vs_cols[:], in_=vs_turned[:, :, 0])
+                gather_keys(g, u)
+            if g == 0:
+                quantize_keys(0)
+        cast_queries(sc, 0)
+        cast_queries(sc, 1)
+        nc.vector.quantize_mx(
+            out=qcodes[:].bitcast(FP8X4), scales=qscales[:], in_=qgrp[:].rearrange("p g q j -> p (g q j)")
+        )
+        quantize_keys(1)
+        score_pass(0)
+        score_pass(1)
+
+        cast(sc, vpool, vraw[0], 0, 0, HALF)
+
+        neg_max = keep.tile([P, 1], F32, name="neg_max")
+        nc.vector.tensor_reduce(out=neg_max[:], in_=scores[:], axis=AXIS.X, op=ALU.max, negate=True)
+        vcut = 256
+        cast(sc, vpool, vraw[1], 1, vcut, HALF)
+        cast(ve, vpool, vraw[1], 1, 0, vcut)
+        p_sb = keep.tile([P, 4, P], F32, name="p_sb")
+        total = keep.tile([P, 1], F32, name="total")
+        nc.scalar.activation(
+            out=p_sb[:],
+            in_=scores[:].rearrange("q (s t) -> q t s", t=4),
+            func=ACT.Exp,
+            bias=neg_max[:],
+            accum_out=total[:],
+        )
+
+        vgot = keep.tile([P, N], U32, name="vgot", align_bytes=64)
+        nc.vector.tensor_copy(
+            out=vgot[:].rearrange("p (t s) -> p s t", t=4),
+            in_=vpool[:].bitcast(U32).indirect(offsets[:]),
+        )
+
+        p_turned = psum.tile([P, 4, P], F32, name="p_turned")
+        for t in range(4):
+            nc.tensor.transpose(p_turned[:, t, :], p_sb[:, t, :], ident32[:])
+
+        v_turned = psum.tile([P, 4, P], F32, name="v_turned")
+        v_words = vgot[:].bitcast(F32).rearrange("p (t s) -> p t s", t=4)
+        for t in range(4):
+            nc.tensor.transpose(v_turned[:, t, :], v_words[:, t, :], ident32[:])
+
+        wgrp = keep.tile([P, NQ, 4], BF16, name="wgrp", align_bytes=64)
+        nc.vector.tensor_tensor(
+            out=wgrp[:],
+            in0=p_turned[:].rearrange("s t q -> s q t"),
+            in1=vs_cols[:].unsqueeze(1).to_broadcast([P, NQ, 4]),
+            op=ALU.mult,
+        )
+        vgrp = keep.tile([P, DV, 4], BF16, name="vgrp", align_bytes=64)
+        v_rows = v_turned[:].rearrange("s t p -> s (t p)").bitcast(BF16).rearrange("s (t e) -> s e t", t=4)
+        wcodes = keep.tile([P, NQ], U32, name="wcodes", align_bytes=64)
+        wscales = keep.tile([P, NQ], U8, name="wscales", align_bytes=64)
+        inv = keep.tile([P, 1], F32, name="inv")
+        nc.vector.reciprocal(out=inv[:], in_=total[:])
+        nc.vector.quantize_mx(out=wcodes[:].bitcast(FP8X4), scales=wscales[:], in_=wgrp[:].rearrange("p q t -> p (q t)"))
+        vcodes = keep.tile([P, DV], U32, name="vcodes", align_bytes=64)
+        vscales = keep.tile([P, DV], U8, name="vscales", align_bytes=64)
+        nc.vector.tensor_copy(out=vgrp[:], in_=v_rows)
+        nc.vector.quantize_mx(out=vcodes[:].bitcast(FP8X4), scales=vscales[:], in_=vgrp[:].rearrange("p e t -> p (e t)"))
+
+        y_ps = psum.tile([P, DV], F32, name="y_ps")
+        nc.tensor.matmul_mx(
+            out=y_ps[:],
+            lhsT=wcodes[:].bitcast(FP8X4),
+            lhsT_scale=wscales[:],
+            rhs=vcodes[:].bitcast(FP8X4),
+            rhs_scale=vscales[:],
+            start=True,
+            stop=True,
+        )
+        y = keep.tile([P, DV], F32, name="y")
+        nc.vector.tensor_scalar(out=y[:], in0=y_ps[:], scalar1=inv[:], scalar2=None, op0=ALU.mult)
+        nc.sync.dma_start(out=out[0], in_=y[:])

@@ -29,7 +29,6 @@ def tile_attend_knn_kernel(tc, qT, kT, vT, vs, offs, out):
         psum = ctx.enter_context(tc.psum_pool(name="psum", bufs=1))
 
         offsets = keep.tile([P, N // 16], U16, name="offsets")
-        nc.sync.dma_start(offsets[:], offs)
 
         warm = keep.tile([P, 1], F32, name="warm")
         warm_out = keep.tile([P, 1], F32, name="warm_out")
@@ -37,10 +36,12 @@ def tile_attend_knn_kernel(tc, qT, kT, vT, vs, offs, out):
         nc.scalar.activation(out=warm_out[:], in_=warm[:], func=ACT.Exp)
 
         vs_pool = keep.tile([P, T], F32, name="vs_pool")
-        nc.gpsimd.memset(vs_pool[:], 0.0)
-        nc.scalar.dma_start(out=vs_pool[0:1, :], in_=vs[0:1, :])
+        nc.gpsimd.memset(vs_pool[:, 0:HALF], 0.0)
+        nc.vector.memset(vs_pool[:, HALF:T], 0.0)
         ident32 = keep.tile([P, P], F32, name="ident32")
         make_identity(nc, ident32[:])
+        ident16 = keep.tile([P, P], BF16, name="ident16")
+        make_identity(nc, ident16[:])
 
         kraw = {}
 
@@ -60,14 +61,22 @@ def tile_attend_knn_kernel(tc, qT, kT, vT, vs, offs, out):
             qraw[g] = raw
 
         vraw = {}
+        v_edges = (0, 704, 1024)
 
         def load_values(h):
-            raw = keep.tile([P, 2, HALF], F32, name=f"vraw_{h}")
-            cols = vT[:, HALF * h : HALF * (h + 1)]
-            nc.sync.dma_start(out=raw[:], in_=cols.rearrange("(p u) n -> p u n", u=2))
+            a, b = v_edges[h], v_edges[h + 1]
+            raw = keep.tile([P, 2, b - a], F32, name=f"vraw_{h}")
+            nc.sync.dma_start(out=raw[:], in_=vT[:, a:b].rearrange("(u p) n -> p u n", u=2))
             vraw[h] = raw
 
+        def cast_values(engine_copy, h):
+            a, b = v_edges[h], v_edges[h + 1]
+            dst = vpool[:, 2 * a : 2 * b].rearrange("p (n e) -> p n e", e=2)
+            engine_copy(out=dst, in_=vraw[h][:].rearrange("p e n -> p n e"))
+
         load_keys(0, 0, 0)
+        nc.sync.dma_start(offsets[:], offs)
+        nc.sync.dma_start(out=vs_pool[0:1, :], in_=vs[0:1, :])
         load_keys(0, 0, 1)
         load_keys(0, 1, 0)
         load_keys(0, 1, 1)
@@ -109,6 +118,14 @@ def tile_attend_knn_kernel(tc, qT, kT, vT, vs, offs, out):
         def cast_queries(engine_copy, g):
             engine_copy(out=qgrp[:, g, :, :], in_=qraw[g][:].rearrange("p j q -> p q j"))
 
+        def quantize_queries(g):
+            cols = slice(NQ * g, NQ * (g + 1))
+            nc.vector.quantize_mx(
+                out=qcodes[:, cols].bitcast(FP8X4),
+                scales=qscales[:, cols],
+                in_=qgrp[:, g, :, :].rearrange("p q j -> p (q j)"),
+            )
+
         def score_pass(g):
             nc.tensor.matmul_mx(
                 out=scores[:],
@@ -129,7 +146,7 @@ def tile_attend_knn_kernel(tc, qT, kT, vT, vs, offs, out):
         vs_by_slot = vs_got[:].rearrange("p (s t) -> p t s", t=4)
         for t in range(4):
             nc.tensor.transpose(vs_turned[:, t, :], vs_by_slot[:, t, :], ident32[:])
-        cuts = {(0, 0, 0): 0, (0, 0, 1): 256, (0, 1, 0): 0, (0, 1, 1): 256, (1, 0, 0): 0, (1, 0, 1): 256, (1, 1, 0): 0, (1, 1, 1): 320}
+        cuts = {(0, 0, 0): 0, (0, 0, 1): 0, (0, 1, 0): 0, (0, 1, 1): 160, (1, 0, 0): 0, (1, 0, 1): 160, (1, 1, 0): 0, (1, 1, 1): 320}
         for g in range(PASSES):
             for u in range(2):
                 for h in range(2):
@@ -145,45 +162,43 @@ def tile_attend_knn_kernel(tc, qT, kT, vT, vs, offs, out):
                 quantize_keys(0)
         cast_queries(sc, 0)
         cast_queries(sc, 1)
-        nc.vector.quantize_mx(
-            out=qcodes[:].bitcast(FP8X4), scales=qscales[:], in_=qgrp[:].rearrange("p g q j -> p (g q j)")
-        )
+        quantize_queries(0)
         quantize_keys(1)
         score_pass(0)
+        quantize_queries(1)
         score_pass(1)
 
-        cast(sc, vpool, vraw[0], 0, 0, HALF)
-
-        neg_max = keep.tile([P, 1], F32, name="neg_max")
-        nc.vector.tensor_reduce(out=neg_max[:], in_=scores[:], axis=AXIS.X, op=ALU.max, negate=True)
-        vcut = 256
-        cast(sc, vpool, vraw[1], 1, vcut, HALF)
-        cast(ve, vpool, vraw[1], 1, 0, vcut)
-        p_sb = keep.tile([P, 4, P], F32, name="p_sb")
-        total = keep.tile([P, 1], F32, name="total")
-        nc.scalar.activation(
-            out=p_sb[:],
-            in_=scores[:].rearrange("q (s t) -> q t s", t=4),
-            func=ACT.Exp,
-            bias=neg_max[:],
-            accum_out=total[:],
-        )
+        cast_values(sc, 0)
+        cast_values(sc, 1)
 
         vgot = keep.tile([P, N], U32, name="vgot", align_bytes=64)
-        nc.vector.tensor_copy(
-            out=vgot[:].rearrange("p (t s) -> p s t", t=4),
-            in_=vpool[:].bitcast(U32).indirect(offsets[:]),
-        )
+        by_slot = vgot[:].rearrange("p (t s) -> p s t", t=4)
 
+        def gather_values(h):
+            nc.vector.tensor_copy(
+                out=by_slot[:, 64 * h : 64 * h + 64, :],
+                in_=vpool[:].bitcast(U32).indirect(offsets[:, 16 * h : 16 * h + 16]),
+            )
+
+        gather_values(0)
+        neg_max = keep.tile([P, 1], F32, name="neg_max")
+        nc.vector.tensor_reduce(out=neg_max[:], in_=scores[:], axis=AXIS.X, op=ALU.max, negate=True)
+        p_sb = keep.tile([P, 4, P], F32, name="p_sb")
+        sums = keep.tile([P, 16], F32, name="sums")
+        by_t = scores[:].rearrange("q (s t) -> q t s", t=4)
         p_turned = psum.tile([P, 4, P], F32, name="p_turned")
-        for t in range(4):
-            nc.tensor.transpose(p_turned[:, t, :], p_sb[:, t, :], ident32[:])
+        for c in range(2):
+            nc.scalar.activation(
+                out=p_sb[:, 2 * c : 2 * c + 2, :],
+                in_=by_t[:, 2 * c : 2 * c + 2, :],
+                func=ACT.Exp,
+                bias=neg_max[:],
+                accum_out=sums[:, 8 * c : 8 * c + 1],
+            )
+            for t in (2 * c, 2 * c + 1):
+                nc.tensor.transpose(p_turned[:, t, :], p_sb[:, t, :], ident32[:])
 
-        v_turned = psum.tile([P, 4, P], F32, name="v_turned")
-        v_words = vgot[:].bitcast(F32).rearrange("p (t s) -> p t s", t=4)
-        for t in range(4):
-            nc.tensor.transpose(v_turned[:, t, :], v_words[:, t, :], ident32[:])
-
+        gather_values(1)
         wgrp = keep.tile([P, NQ, 4], BF16, name="wgrp", align_bytes=64)
         nc.vector.tensor_tensor(
             out=wgrp[:],
@@ -191,28 +206,34 @@ def tile_attend_knn_kernel(tc, qT, kT, vT, vs, offs, out):
             in1=vs_cols[:].unsqueeze(1).to_broadcast([P, NQ, 4]),
             op=ALU.mult,
         )
-        vgrp = keep.tile([P, DV, 4], BF16, name="vgrp", align_bytes=64)
-        v_rows = v_turned[:].rearrange("s t p -> s (t p)").bitcast(BF16).rearrange("s (t e) -> s e t", t=4)
+        total = keep.tile([P, 1], F32, name="total")
+        nc.vector.tensor_tensor(out=total[:], in0=sums[:, 0:1], in1=sums[:, 8:9], op=ALU.add)
         wcodes = keep.tile([P, NQ], U32, name="wcodes", align_bytes=64)
         wscales = keep.tile([P, NQ], U8, name="wscales", align_bytes=64)
+        nc.vector.quantize_mx(out=wcodes[:].bitcast(FP8X4), scales=wscales[:], in_=wgrp[:].rearrange("p q t -> p (q t)"))
         inv = keep.tile([P, 1], F32, name="inv")
         nc.vector.reciprocal(out=inv[:], in_=total[:])
-        nc.vector.quantize_mx(out=wcodes[:].bitcast(FP8X4), scales=wscales[:], in_=wgrp[:].rearrange("p q t -> p (q t)"))
-        vcodes = keep.tile([P, DV], U32, name="vcodes", align_bytes=64)
-        vscales = keep.tile([P, DV], U8, name="vscales", align_bytes=64)
-        nc.vector.tensor_copy(out=vgrp[:], in_=v_rows)
-        nc.vector.quantize_mx(out=vcodes[:].bitcast(FP8X4), scales=vscales[:], in_=vgrp[:].rearrange("p e t -> p (e t)"))
 
-        y_ps = psum.tile([P, DV], F32, name="y_ps")
-        nc.tensor.matmul_mx(
-            out=y_ps[:],
-            lhsT=wcodes[:].bitcast(FP8X4),
-            lhsT_scale=wscales[:],
-            rhs=vcodes[:].bitcast(FP8X4),
-            rhs_scale=vscales[:],
-            start=True,
-            stop=True,
-        )
-        y = keep.tile([P, DV], F32, name="y")
-        nc.vector.tensor_scalar(out=y[:], in0=y_ps[:], scalar1=inv[:], scalar2=None, op0=ALU.mult)
-        nc.sync.dma_start(out=out[0], in_=y[:])
+        v_halves = vgot[:].bitcast(BF16).rearrange("p (t s u) -> p t u s", t=4, u=2)
+        for u in range(2):
+            v_turned = psum.tile([P, 4, P], BF16, name=f"v_turned_{u}")
+            for t in range(4):
+                nc.tensor.transpose(v_turned[:, t, :], v_halves[:, t, u, :], ident16[:])
+            vgrp = keep.tile([P, P, 4], BF16, name=f"vgrp_{u}", align_bytes=64)
+            (sc, ve)[u](out=vgrp[:], in_=v_turned[:].rearrange("s t e -> s e t"))
+            vcodes = keep.tile([P, P], U32, name=f"vcodes_{u}", align_bytes=64)
+            vscales = keep.tile([P, P], U8, name=f"vscales_{u}", align_bytes=64)
+            nc.vector.quantize_mx(out=vcodes[:].bitcast(FP8X4), scales=vscales[:], in_=vgrp[:].rearrange("p e t -> p (e t)"))
+            y_ps = psum.tile([P, P], F32, name=f"y_ps_{u}")
+            nc.tensor.matmul_mx(
+                out=y_ps[:],
+                lhsT=wcodes[:].bitcast(FP8X4),
+                lhsT_scale=wscales[:],
+                rhs=vcodes[:].bitcast(FP8X4),
+                rhs_scale=vscales[:],
+                start=True,
+                stop=True,
+            )
+            y = keep.tile([P, P], F32, name=f"y_{u}")
+            nc.vector.tensor_scalar(out=y[:], in0=y_ps[:], scalar1=inv[:], scalar2=None, op0=ALU.mult)
+            nc.sync.dma_start(out=out[0, :, P * u : P * (u + 1)], in_=y[:])

@@ -40,50 +40,48 @@ def tile_attend_knn_kernel(tc, qT, kT, vT, vs, offs, out):
         nc.vector.memset(vs_pool[:, HALF:T], 0.0)
         ident32 = keep.tile([P, P], F32, name="ident32")
         make_identity(nc, ident32[:])
-        ident16 = keep.tile([P, P], BF16, name="ident16")
-        make_identity(nc, ident16[:])
 
         kraw = {}
 
-        def load_keys(g, u, h):
-            raw = keep.tile([P, 2, HALF], F32, name=f"kraw_{g}_{u}_{h}")
-            rows = kT[512 * g : 512 * (g + 1), HALF * h : HALF * (h + 1)]
+        def load_keys(g, u, a, b):
+            raw = keep.tile([P, 2, b - a], F32, name=f"kraw_{g}_{u}_{a}")
+            rows = kT[512 * g : 512 * (g + 1), a:b]
             rows = rows.rearrange("(p u e) n -> p u e n", u=2, e=2)
             nc.sync.dma_start(out=raw[:], in_=rows[:, u, :, :])
-            kraw[g, u, h] = raw
+            kraw[g, u, a] = raw
 
         qraw = {}
 
         def load_queries(g):
-            raw = keep.tile([P, 4, NQ], F32, name=f"qraw_{g}")
+            raw = keep.tile([P, 4, NQ], F32, name=f"qraw_{g}", tag=f"q_then_k_{g}", align_bytes=64)
             rows = qT[0, 512 * g : 512 * (g + 1), :]
             nc.sync.dma_start(out=raw[:], in_=rows.rearrange("(p j) q -> p j q", j=4))
             qraw[g] = raw
 
         vraw = {}
-        v_edges = (0, 704, 1024)
+        v_edges = (0, 512, 1024)
 
         def load_values(h):
             a, b = v_edges[h], v_edges[h + 1]
             raw = keep.tile([P, 2, b - a], F32, name=f"vraw_{h}")
-            nc.sync.dma_start(out=raw[:], in_=vT[:, a:b].rearrange("(u p) n -> p u n", u=2))
+            nc.sync.dma_start(out=raw[:], in_=vT[:, a:b].rearrange("(p u) n -> p u n", u=2))
             vraw[h] = raw
 
-        def cast_values(engine_copy, h):
-            a, b = v_edges[h], v_edges[h + 1]
+        def cast_values(engine_copy, h, a, b):
+            base = v_edges[h]
             dst = vpool[:, 2 * a : 2 * b].rearrange("p (n e) -> p n e", e=2)
-            engine_copy(out=dst, in_=vraw[h][:].rearrange("p e n -> p n e"))
+            engine_copy(out=dst, in_=vraw[h][:, :, a - base : b - base].rearrange("p e n -> p n e"))
 
-        load_keys(0, 0, 0)
+        load_keys(0, 0, 0, 512)
         nc.sync.dma_start(offsets[:], offs)
         nc.sync.dma_start(out=vs_pool[0:1, :], in_=vs[0:1, :])
-        load_keys(0, 0, 1)
-        load_keys(0, 1, 0)
-        load_keys(0, 1, 1)
-        load_keys(1, 0, 0)
-        load_keys(1, 0, 1)
-        load_keys(1, 1, 0)
-        load_keys(1, 1, 1)
+        load_keys(0, 0, 512, 1024)
+        load_keys(0, 1, 0, 512)
+        load_keys(0, 1, 512, 1024)
+        load_keys(1, 0, 0, 512)
+        load_keys(1, 0, 512, 1024)
+        load_keys(1, 1, 0, 512)
+        load_keys(1, 1, 512, 1024)
         load_queries(0)
         load_queries(1)
         load_values(0)
@@ -95,12 +93,12 @@ def tile_attend_knn_kernel(tc, qT, kT, vT, vs, offs, out):
                 kpool[g, u] = keep.tile([P, 2 * T], BF16, name=f"kpool_{g}_{u}", align_bytes=64)
         vpool = keep.tile([P, 2 * T], BF16, name="vpool", align_bytes=64)
 
-        def cast(engine_copy, pool, raw, h, a, b):
-            dst = pool[:, 2 * (HALF * h + a) : 2 * (HALF * h + b)]
-            engine_copy(out=dst.rearrange("p (n e) -> p n e", e=2), in_=raw[:, :, a:b].rearrange("p e n -> p n e"))
+        def cast(engine_copy, pool, raw, base, a, b):
+            dst = pool[:, 2 * a : 2 * b].rearrange("p (n e) -> p n e", e=2)
+            engine_copy(out=dst, in_=raw[:, :, a - base : b - base].rearrange("p e n -> p n e"))
 
         kgrp = [keep.tile([P, 4 * N], BF16, name=f"kgrp_{g}", align_bytes=64) for g in range(PASSES)]
-        kcodes = [keep.tile([P, N], U32, name=f"kcodes_{g}", align_bytes=64) for g in range(PASSES)]
+        kcodes = [keep.tile([P, N], U32, name=f"kcodes_{g}", tag=("kcodes_0", "q_then_k_1")[g], align_bytes=64) for g in range(PASSES)]
         kscales = [keep.tile([P, N], U8, name=f"kscales_{g}", align_bytes=64) for g in range(PASSES)]
 
         def gather_keys(g, u):
@@ -117,14 +115,6 @@ def tile_attend_knn_kernel(tc, qT, kT, vT, vs, offs, out):
 
         def cast_queries(engine_copy, g):
             engine_copy(out=qgrp[:, g, :, :], in_=qraw[g][:].rearrange("p j q -> p q j"))
-
-        def quantize_queries(g):
-            cols = slice(NQ * g, NQ * (g + 1))
-            nc.vector.quantize_mx(
-                out=qcodes[:, cols].bitcast(FP8X4),
-                scales=qscales[:, cols],
-                in_=qgrp[:, g, :, :].rearrange("p q j -> p (q j)"),
-            )
 
         def score_pass(g):
             nc.tensor.matmul_mx(
@@ -146,41 +136,41 @@ def tile_attend_knn_kernel(tc, qT, kT, vT, vs, offs, out):
         vs_by_slot = vs_got[:].rearrange("p (s t) -> p t s", t=4)
         for t in range(4):
             nc.tensor.transpose(vs_turned[:, t, :], vs_by_slot[:, t, :], ident32[:])
-        cuts = {(0, 0, 0): 0, (0, 0, 1): 0, (0, 1, 0): 0, (0, 1, 1): 160, (1, 0, 0): 0, (1, 0, 1): 160, (1, 1, 0): 0, (1, 1, 1): 320}
-        for g in range(PASSES):
-            for u in range(2):
-                for h in range(2):
-                    cut = cuts[g, u, h]
-                    if cut < HALF:
-                        cast(sc, kpool[g, u], kraw[g, u, h], h, cut, HALF)
-                    if cut > 0:
-                        cast(ve, kpool[g, u], kraw[g, u, h], h, 0, cut)
-                if (g, u) == (0, 1):
-                    nc.vector.tensor_copy(out=vs_cols[:], in_=vs_turned[:, :, 0])
-                gather_keys(g, u)
-            if g == 0:
-                quantize_keys(0)
+        cast(sc, kpool[0, 0], kraw[0, 0, 0], 0, 0, 512)
+        cast(sc, kpool[0, 0], kraw[0, 0, 512], 512, 768, 1024)
+        cast(ve, kpool[0, 0], kraw[0, 0, 512], 512, 512, 768)
+        gather_keys(0, 0)
+        cast(sc, kpool[0, 1], kraw[0, 1, 0], 0, 0, 512)
+        cast(sc, kpool[0, 1], kraw[0, 1, 512], 512, 672, 1024)
+        cast(ve, kpool[0, 1], kraw[0, 1, 512], 512, 512, 672)
+        nc.vector.tensor_copy(out=vs_cols[:], in_=vs_turned[:, :, 0])
+        gather_keys(0, 1)
+        quantize_keys(0)
+        cast(sc, kpool[1, 0], kraw[1, 0, 0], 0, 0, 512)
+        cast(sc, kpool[1, 0], kraw[1, 0, 512], 512, 512, 1024)
+        gather_keys(1, 0)
+        cast(sc, kpool[1, 1], kraw[1, 1, 0], 0, 0, 512)
+        cast(sc, kpool[1, 1], kraw[1, 1, 512], 512, 768, 1024)
+        cast(ve, kpool[1, 1], kraw[1, 1, 512], 512, 512, 768)
+        gather_keys(1, 1)
         cast_queries(sc, 0)
         cast_queries(sc, 1)
-        quantize_queries(0)
+        nc.vector.quantize_mx(
+            out=qcodes[:].bitcast(FP8X4), scales=qscales[:], in_=qgrp[:].rearrange("p g q j -> p (g q j)")
+        )
         quantize_keys(1)
         score_pass(0)
-        quantize_queries(1)
         score_pass(1)
 
-        cast_values(sc, 0)
-        cast_values(sc, 1)
+        cast_values(sc, 0, 0, 512)
+        cast_values(sc, 1, 512, 1024)
 
         vgot = keep.tile([P, N], U32, name="vgot", align_bytes=64)
         by_slot = vgot[:].rearrange("p (t s) -> p s t", t=4)
 
-        def gather_values(h):
-            nc.vector.tensor_copy(
-                out=by_slot[:, 64 * h : 64 * h + 64, :],
-                in_=vpool[:].bitcast(U32).indirect(offsets[:, 16 * h : 16 * h + 16]),
-            )
+        def gather_values():
+            nc.vector.tensor_copy(out=by_slot, in_=vpool[:].bitcast(U32).indirect(offsets[:]))
 
-        gather_values(0)
         neg_max = keep.tile([P, 1], F32, name="neg_max")
         nc.vector.tensor_reduce(out=neg_max[:], in_=scores[:], axis=AXIS.X, op=ALU.max, negate=True)
         p_sb = keep.tile([P, 4, P], F32, name="p_sb")
@@ -198,7 +188,7 @@ def tile_attend_knn_kernel(tc, qT, kT, vT, vs, offs, out):
             for t in (2 * c, 2 * c + 1):
                 nc.tensor.transpose(p_turned[:, t, :], p_sb[:, t, :], ident32[:])
 
-        gather_values(1)
+        gather_values()
         wgrp = keep.tile([P, NQ, 4], BF16, name="wgrp", align_bytes=64)
         nc.vector.tensor_tensor(
             out=wgrp[:],
@@ -214,13 +204,14 @@ def tile_attend_knn_kernel(tc, qT, kT, vT, vs, offs, out):
         inv = keep.tile([P, 1], F32, name="inv")
         nc.vector.reciprocal(out=inv[:], in_=total[:])
 
-        v_halves = vgot[:].bitcast(BF16).rearrange("p (t s u) -> p t u s", t=4, u=2)
+        v_turned = psum.tile([P, 4 * P], F32, name="v_turned")
+        v_words = vgot[:].bitcast(F32)
+        for t in range(4):
+            nc.tensor.transpose(v_turned[:, P * t : P * (t + 1)], v_words[:, P * t : P * (t + 1)], ident32[:])
+        v_rows = v_turned[:].bitcast(BF16).rearrange("s (t e) -> s e t", t=4)
         for u in range(2):
-            v_turned = psum.tile([P, 4, P], BF16, name=f"v_turned_{u}")
-            for t in range(4):
-                nc.tensor.transpose(v_turned[:, t, :], v_halves[:, t, u, :], ident16[:])
             vgrp = keep.tile([P, P, 4], BF16, name=f"vgrp_{u}", align_bytes=64)
-            (sc, ve)[u](out=vgrp[:], in_=v_turned[:].rearrange("s t e -> s e t"))
+            nc.scalar.copy(out=vgrp[:], in_=v_rows[:, P * u : P * (u + 1), :])
             vcodes = keep.tile([P, P], U32, name=f"vcodes_{u}", align_bytes=64)
             vscales = keep.tile([P, P], U8, name=f"vscales_{u}", align_bytes=64)
             nc.vector.quantize_mx(out=vcodes[:].bitcast(FP8X4), scales=vscales[:], in_=vgrp[:].rearrange("p e t -> p (e t)"))

@@ -59,7 +59,7 @@ def tile_attend_knn_kernel(tc, qT, kT, vT, vs, offs, out):
             qraw[g] = raw
 
         vraw = {}
-        v_edges = (0, 512, 1024)
+        v_edges = (0, 640, 1024)
 
         def load_values(h):
             a, b = v_edges[h], v_edges[h + 1]
@@ -141,17 +141,16 @@ def tile_attend_knn_kernel(tc, qT, kT, vT, vs, offs, out):
         cast(ve, kpool[0, 0], kraw[0, 0, 512], 512, 512, 768)
         gather_keys(0, 0)
         cast(sc, kpool[0, 1], kraw[0, 1, 0], 0, 0, 512)
-        cast(sc, kpool[0, 1], kraw[0, 1, 512], 512, 672, 1024)
-        cast(ve, kpool[0, 1], kraw[0, 1, 512], 512, 512, 672)
-        nc.vector.tensor_copy(out=vs_cols[:], in_=vs_turned[:, :, 0])
+        cast(sc, kpool[0, 1], kraw[0, 1, 512], 512, 512, 1024)
+        nc.scalar.copy(out=vs_cols[:], in_=vs_turned[:, :, 0])
         gather_keys(0, 1)
         quantize_keys(0)
         cast(sc, kpool[1, 0], kraw[1, 0, 0], 0, 0, 512)
         cast(sc, kpool[1, 0], kraw[1, 0, 512], 512, 512, 1024)
         gather_keys(1, 0)
         cast(sc, kpool[1, 1], kraw[1, 1, 0], 0, 0, 512)
-        cast(sc, kpool[1, 1], kraw[1, 1, 512], 512, 768, 1024)
-        cast(ve, kpool[1, 1], kraw[1, 1, 512], 512, 512, 768)
+        cast(sc, kpool[1, 1], kraw[1, 1, 512], 512, 736, 1024)
+        cast(ve, kpool[1, 1], kraw[1, 1, 512], 512, 512, 736)
         gather_keys(1, 1)
         cast_queries(sc, 0)
         cast_queries(sc, 1)
@@ -162,8 +161,8 @@ def tile_attend_knn_kernel(tc, qT, kT, vT, vs, offs, out):
         score_pass(0)
         score_pass(1)
 
-        cast_values(sc, 0, 0, 512)
-        cast_values(sc, 1, 512, 1024)
+        cast_values(sc, 0, 0, 640)
+        cast_values(sc, 1, 640, 1024)
 
         vgot = keep.tile([P, N], U32, name="vgot", align_bytes=64)
         by_slot = vgot[:].rearrange("p (t s) -> p s t", t=4)
@@ -174,18 +173,18 @@ def tile_attend_knn_kernel(tc, qT, kT, vT, vs, offs, out):
         neg_max = keep.tile([P, 1], F32, name="neg_max")
         nc.vector.tensor_reduce(out=neg_max[:], in_=scores[:], axis=AXIS.X, op=ALU.max, negate=True)
         p_sb = keep.tile([P, 4, P], F32, name="p_sb")
-        sums = keep.tile([P, 16], F32, name="sums")
+        sums = keep.tile([P, 3], F32, name="sums")
         by_t = scores[:].rearrange("q (s t) -> q t s", t=4)
         p_turned = psum.tile([P, 4, P], F32, name="p_turned")
-        for c in range(2):
+        for c, (first, last) in enumerate(((0, 2), (2, 3), (3, 4))):
             nc.scalar.activation(
-                out=p_sb[:, 2 * c : 2 * c + 2, :],
-                in_=by_t[:, 2 * c : 2 * c + 2, :],
+                out=p_sb[:, first:last, :],
+                in_=by_t[:, first:last, :],
                 func=ACT.Exp,
                 bias=neg_max[:],
-                accum_out=sums[:, 8 * c : 8 * c + 1],
+                accum_out=sums[:, c : c + 1],
             )
-            for t in (2 * c, 2 * c + 1):
+            for t in range(first, last):
                 nc.tensor.transpose(p_turned[:, t, :], p_sb[:, t, :], ident32[:])
 
         gather_values()
@@ -197,7 +196,7 @@ def tile_attend_knn_kernel(tc, qT, kT, vT, vs, offs, out):
             op=ALU.mult,
         )
         total = keep.tile([P, 1], F32, name="total")
-        nc.vector.tensor_tensor(out=total[:], in0=sums[:, 0:1], in1=sums[:, 8:9], op=ALU.add)
+        nc.vector.tensor_reduce(out=total[:], in_=sums[:], axis=AXIS.X, op=ALU.add)
         wcodes = keep.tile([P, NQ], U32, name="wcodes", align_bytes=64)
         wscales = keep.tile([P, NQ], U8, name="wscales", align_bytes=64)
         nc.vector.quantize_mx(out=wcodes[:].bitcast(FP8X4), scales=wscales[:], in_=wgrp[:].rearrange("p q t -> p (q t)"))
@@ -226,5 +225,8 @@ def tile_attend_knn_kernel(tc, qT, kT, vT, vs, offs, out):
                 stop=True,
             )
             y = keep.tile([P, P], F32, name=f"y_{u}")
-            nc.vector.tensor_scalar(out=y[:], in0=y_ps[:], scalar1=inv[:], scalar2=None, op0=ALU.mult)
+            if u == 0:
+                nc.scalar.activation(out=y[:], in_=y_ps[:], func=ACT.Copy, scale=inv[:])
+            else:
+                nc.vector.tensor_scalar(out=y[:], in0=y_ps[:], scalar1=inv[:], scalar2=None, op0=ALU.mult)
             nc.sync.dma_start(out=out[0, :, P * u : P * (u + 1)], in_=y[:])

from contextlib import ExitStack

import concourse.mybir as mybir
from concourse.masks import make_identity

F32 = mybir.dt.float32
BF16 = mybir.dt.bfloat16
U32 = mybir.dt.uint32
U16 = mybir.dt.uint16
U8 = mybir.dt.uint8
FP8X4 = mybir.dt.float8_e4m3fn_x4
ACT = mybir.ActivationFunctionType
ALU = mybir.AluOpType
AXIS = mybir.AxisListType

P = 128
N, T, DK, DV, NQ = 512, 1024, 1024, 256, 128
PASSES = DK // 512
HALF = T // 2

FLOPS = 2 * NQ * N * (DK + DV)
BYTES = 4 * (DK * NQ + DK * T + DV * T + T + NQ * DV) + 2 * P * N // 16


def tile_attend_knn_kernel(tc, qT, kT, vT, vs, offs, out):
    nc = tc.nc
    with ExitStack() as ctx:
        keep = ctx.enter_context(tc.tile_pool(name="keep", bufs=1))
        psum = ctx.enter_context(tc.psum_pool(name="psum", bufs=1))

        offsets = keep.tile([P, N // 16], U16, name="offsets")

        warm = keep.tile([P, 1], F32, name="warm")
        warm_out = keep.tile([P, 1], F32, name="warm_out")
        nc.vector.memset(warm[:], 0.0)
        nc.scalar.activation(out=warm_out[:], in_=warm[:], func=ACT.Exp)

        vs_pool = keep.tile([P, T], F32, name="vs_pool")
        nc.gpsimd.memset(vs_pool[:, 0:HALF], 0.0)
        nc.vector.memset(vs_pool[:, HALF:T], 0.0)
        ident32 = keep.tile([P, P], F32, name="ident32")
        make_identity(nc, ident32[:])

        kraw = {}

        def load_keys(g, u, a, b):
            raw = keep.tile([P, 2, b - a], F32, name=f"kraw_{g}_{u}_{a}")
            rows = kT[512 * g : 512 * (g + 1), a:b]
            rows = rows.rearrange("(p u e) n -> p u e n", u=2, e=2)
            nc.sync.dma_start(out=raw[:], in_=rows[:, u, :, :])
            kraw[g, u, a] = raw

        qraw = {}

        def load_queries(g):
            raw = keep.tile([P, 4, NQ], F32, name=f"qraw_{g}", tag=f"q_then_k_{g}", align_bytes=64)
            rows = qT[0, 512 * g : 512 * (g + 1), :]
            nc.sync.dma_start(out=raw[:], in_=rows.rearrange("(p j) q -> p j q", j=4))
            qraw[g] = raw

        vraw = {}
        v_edges = (0, 640, 1024)

        def load_values(h):
            a, b = v_edges[h], v_edges[h + 1]
            raw = keep.tile([P, 2, b - a], F32, name=f"vraw_{h}")
            nc.sync.dma_start(out=raw[:], in_=vT[:, a:b].rearrange("(p u) n -> p u n", u=2))
            vraw[h] = raw

        def cast_values(engine_copy, h, a, b):
            base = v_edges[h]
            dst = vpool[:, 2 * a : 2 * b].rearrange("p (n e) -> p n e", e=2)
            engine_copy(out=dst, in_=vraw[h][:, :, a - base : b - base].rearrange("p e n -> p n e"))

        load_keys(0, 0, 0, 512)
        nc.sync.dma_start(offsets[:], offs)
        nc.sync.dma_start(out=vs_pool[0:1, :], in_=vs[0:1, :])
        load_keys(0, 0, 512, 1024)
        load_keys(0, 1, 0, 512)
        load_keys(0, 1, 512, 1024)
        load_keys(1, 0, 0, 512)
        load_keys(1, 0, 512, 1024)
        load_keys(1, 1, 0, 512)
        load_keys(1, 1, 512, 1024)
        load_queries(0)
        load_queries(1)
        load_values(0)
        load_values(1)

        kpool = {}
        for g in range(PASSES):
            for u in range(2):
                kpool[g, u] = keep.tile([P, 2 * T], BF16, name=f"kpool_{g}_{u}", align_bytes=64)
        vpool = keep.tile([P, 2 * T], BF16, name="vpool", align_bytes=64)

        def cast(engine_copy, pool, raw, base, a, b):
            dst = pool[:, 2 * a : 2 * b].rearrange("p (n e) -> p n e", e=2)
            engine_copy(out=dst, in_=raw[:, :, a - base : b - base].rearrange("p e n -> p n e"))

        kgrp = [keep.tile([P, 4 * N], BF16, name=f"kgrp_{g}", align_bytes=64) for g in range(PASSES)]
        kcodes = [keep.tile([P, N], U32, name=f"kcodes_{g}", tag=("kcodes_0", "q_then_k_1")[g], align_bytes=64) for g in range(PASSES)]
        kscales = [keep.tile([P, N], U8, name=f"kscales_{g}", align_bytes=64) for g in range(PASSES)]

        def gather_keys(g, u):
            words = kgrp[g][:].bitcast(U32).rearrange("p (n u) -> p n u", u=2)
            nc.vector.tensor_copy(out=words[:, :, u], in_=kpool[g, u][:].bitcast(U32).indirect(offsets[:]))

        def quantize_keys(g):
            nc.vector.quantize_mx(out=kcodes[g][:].bitcast(FP8X4), scales=kscales[g][:], in_=kgrp[g][:])

        scores = psum.tile([P, N], F32, name="scores")
        qcodes = keep.tile([P, PASSES * NQ], U32, name="qcodes", align_bytes=64)
        qscales = keep.tile([P, PASSES * NQ], U8, name="qscales", align_bytes=64)
        qgrp = keep.tile([P, PASSES, NQ, 4], BF16, name="qgrp", align_bytes=64)

        def cast_queries(engine_copy, g):
            engine_copy(out=qgrp[:, g, :, :], in_=qraw[g][:].rearrange("p j q -> p q j"))

        def score_pass(g):
            nc.tensor.matmul_mx(
                out=scores[:],
                lhsT=qcodes[:, NQ * g : NQ * (g + 1)].bitcast(FP8X4),
                lhsT_scale=qscales[:, NQ * g : NQ * (g + 1)],
                rhs=kcodes[g][:].bitcast(FP8X4),
                rhs_scale=kscales[g][:],
                start=(g == 0),
                stop=(g == PASSES - 1),
            )

        sc, ve = nc.scalar.copy, nc.vector.tensor_copy
        vs_got = keep.tile([P, N], F32, name="vs_got")
        vs_cols = keep.tile([P, 4], F32, name="vs_cols")
        vs_turned = psum.tile([P, 4, P], F32, name="vs_turned")

        nc.vector.tensor_copy(out=vs_got[:], in_=vs_pool[:].indirect(offsets[:]))
        vs_by_slot = vs_got[:].rearrange("p (s t) -> p t s", t=4)
        for t in range(4):
            nc.tensor.transpose(vs_turned[:, t, :], vs_by_slot[:, t, :], ident32[:])
        cast(sc, kpool[0, 0], kraw[0, 0, 0], 0, 0, 512)
        cast(sc, kpool[0, 0], kraw[0, 0, 512], 512, 768, 1024)
        cast(ve, kpool[0, 0], kraw[0, 0, 512], 512, 512, 768)
        gather_keys(0, 0)
        cast(sc, kpool[0, 1], kraw[0, 1, 0], 0, 0, 512)
        cast(sc, kpool[0, 1], kraw[0, 1, 512], 512, 512, 1024)
        nc.scalar.copy(out=vs_cols[:], in_=vs_turned[:, :, 0])
        gather_keys(0, 1)
        quantize_keys(0)
        cast(sc, kpool[1, 0], kraw[1, 0, 0], 0, 0, 512)
        cast(sc, kpool[1, 0], kraw[1, 0, 512], 512, 512, 1024)
        gather_keys(1, 0)
        cast(sc, kpool[1, 1], kraw[1, 1, 0], 0, 0, 512)
        cast(sc, kpool[1, 1], kraw[1, 1, 512], 512, 736, 1024)
        cast(ve, kpool[1, 1], kraw[1, 1, 512], 512, 512, 736)
        gather_keys(1, 1)
        cast_queries(sc, 0)
        cast_queries(sc, 1)
        nc.vector.quantize_mx(
            out=qcodes[:].bitcast(FP8X4), scales=qscales[:], in_=qgrp[:].rearrange("p g q j -> p (g q j)")
        )
        quantize_keys(1)
        score_pass(0)
        score_pass(1)

        cast_values(sc, 0, 0, 640)
        cast_values(sc, 1, 640, 1024)

        vgot = keep.tile([P, N], U32, name="vgot", align_bytes=64)
        by_slot = vgot[:].rearrange("p (t s) -> p s t", t=4)

        def gather_values():
            nc.vector.tensor_copy(out=by_slot, in_=vpool[:].bitcast(U32).indirect(offsets[:]))

        neg_max = keep.tile([P, 1], F32, name="neg_max")
        nc.vector.tensor_reduce(out=neg_max[:], in_=scores[:], axis=AXIS.X, op=ALU.max, negate=True)
        p_sb = keep.tile([P, 4, P], F32, name="p_sb")
        sums = keep.tile([P, 3], F32, name="sums")
        by_t = scores[:].rearrange("q (s t) -> q t s", t=4)
        p_turned = psum.tile([P, 4, P], F32, name="p_turned")
        for c, (first, last) in enumerate(((0, 2), (2, 3), (3, 4))):
            nc.scalar.activation(
                out=p_sb[:, first:last, :],
                in_=by_t[:, first:last, :],
                func=ACT.Exp,
                bias=neg_max[:],
                accum_out=sums[:, c : c + 1],
            )
            for t in range(first, last):
                nc.tensor.transpose(p_turned[:, t, :], p_sb[:, t, :], ident32[:])

        gather_values()
        wgrp = keep.tile([P, NQ, 4], BF16, name="wgrp", align_bytes=64)
        nc.vector.tensor_tensor(
            out=wgrp[:],
            in0=p_turned[:].rearrange("s t q -> s q t"),
            in1=vs_cols[:].unsqueeze(1).to_broadcast([P, NQ, 4]),
            op=ALU.mult,
        )
        total = keep.tile([P, 1], F32, name="total")
        nc.vector.tensor_reduce(out=total[:], in_=sums[:], axis=AXIS.X, op=ALU.add)
        wcodes = keep.tile([P, NQ], U32, name="wcodes", align_bytes=64)
        wscales = keep.tile([P, NQ], U8, name="wscales", align_bytes=64)
        nc.vector.quantize_mx(out=wcodes[:].bitcast(FP8X4), scales=wscales[:], in_=wgrp[:].rearrange("p q t -> p (q t)"))
        inv = keep.tile([P, 1], F32, name="inv")
        nc.vector.reciprocal(out=inv[:], in_=total[:])

        v_turned = psum.tile([P, 4 * P], F32, name="v_turned")
        v_words = vgot[:].bitcast(F32)
        for t in range(4):
            nc.tensor.transpose(v_turned[:, P * t : P * (t + 1)], v_words[:, P * t : P * (t + 1)], ident32[:])
        v_rows = v_turned[:].bitcast(BF16).rearrange("s (t e) -> s e t", t=4)
        for u in range(2):
            vgrp = keep.tile([P, P, 4], BF16, name=f"vgrp_{u}", align_bytes=64)
            nc.scalar.copy(out=vgrp[:], in_=v_rows[:, P * u : P * (u + 1), :])
            vcodes = keep.tile([P, P], U32, name=f"vcodes_{u}", align_bytes=64)
            vscales = keep.tile([P, P], U8, name=f"vscales_{u}", align_bytes=64)
            nc.vector.quantize_mx(out=vcodes[:].bitcast(FP8X4), scales=vscales[:], in_=vgrp[:].rearrange("p e t -> p (e t)"))
            y_ps = psum.tile([P, P], F32, name=f"y_ps_{u}")
            nc.tensor.matmul_mx(
                out=y_ps[:],
                lhsT=wcodes[:].bitcast(FP8X4),
                lhsT_scale=wscales[:],
                rhs=vcodes[:].bitcast(FP8X4),
                rhs_scale=vscales[:],
                start=True,
                stop=True,
            )
            y = keep.tile([P, P], F32, name=f"y_{u}")
            if u == 0:
                nc.scalar.activation(out=y[:], in_=y_ps[:], func=ACT.Copy, scale=inv[:])
            else:
                nc.vector.tensor_scalar(out=y[:], in0=y_ps[:], scalar1=inv[:], scalar2=None, op0=ALU.mult)
            nc.sync.dma_start(out=out[0, :, P * u : P * (u + 1)], in_=y[:])
